import numpy as np
import ml_dtypes


def mxq(x, axis, fmt="e4m3"):
    dtype, down = {"e4m3": (ml_dtypes.float8_e4m3fn, 7), "e5m2": (ml_dtypes.float8_e5m2, 14)}[fmt]
    v = np.moveaxis(np.asarray(x, np.float32).astype(ml_dtypes.bfloat16).astype(np.float64), axis, -1)
    blocks = v.reshape(v.shape[:-1] + (-1, 32))
    amax = np.abs(blocks).max(-1, keepdims=True)
    byte = np.maximum(np.where(amax > 0, np.frexp(amax)[1] - 1 + 127, 0) - down, 1)
    scale = np.exp2(byte - 127.0)
    codes = (blocks / scale).astype(np.float32).astype(dtype).astype(np.float64)
    return np.moveaxis((codes * scale).reshape(v.shape), -1, axis)


WIDE = False


def mx_kscale(k, group=512):
    if not WIDE:
        return np.ones(k)
    levels = np.array([10, -10, 5, -5, 0])
    if group != 512:
        return np.exp2(np.random.permutation(np.resize(levels, k // group))).repeat(group)
    if k % 512:
        return np.exp2(np.random.permutation(np.resize(levels, k // 32))).repeat(32)
    a = np.empty((k // 512, 16))
    for p in range(k // 512):
        a[p, :8] = np.random.permutation(np.resize(levels, 8))
        for g in range(8):
            far = levels[np.abs(levels - a[p, g]) >= 10]
            a[p, g + 8] = far[np.random.randint(len(far))]
    return np.exp2(a.ravel()).repeat(32)


def f64(x):
    return np.asarray(x).astype(np.float64)


H, D, N = 4, 256, 1024


def setup_inputs():
    n = np.random.standard_normal
    s = mx_kscale(D, 0)[:, None]
    S = n((H, D, 128))
    S[:, :, 127] = np.random.uniform(0.5, 1.5, (H, D))
    return {
        "q": n((H, D, N)).astype(np.float32),
        "qa": (np.random.uniform(0.5, 2.0, (D, 1)) * s).astype(np.float32),
        "S": (S / s).astype(np.float32),
    }


def reference(q, qa, S):
    fq = (np.maximum(f64(q), 0.0) + 0.125) * f64(qa)
    y = mxq(fq, 1, "e4m3").transpose(0, 2, 1) @ mxq(f64(S), 1, "e4m3")
    y = y / y[:, :, 127:128]
    return y

@@ -1,0 +1,215 @@
+from contextlib import ExitStack
+
+import concourse.mybir as mybir
+
+H, D, N, E = 4, 256, 1024, 128
+FLOPS = 2 * H * N * D * E
+
+F32 = mybir.dt.float32
+BF16 = mybir.dt.bfloat16
+U32 = mybir.dt.uint32
+U8 = mybir.dt.uint8
+FP8X4 = mybir.dt.float8_e4m3fn_x4
+ALU = mybir.AluOpType
+ACT = mybir.ActivationFunctionType
+
+P = 128
+PACK = 4
+ROWS = D // PACK
+SIDE = P // ROWS
+PAIRS = H // SIDE
+CHUNK = 512
+DEAL = CHUNK // P
+CHUNKS = PAIRS * (N // CHUNK)
+OFFSET = 0.125
+FAR = 1.5e38
+
+
+def tile_rows_read_relu1_norm_kernel(tc, q, qa, S, out):
+    nc = tc.nc
+    with ExitStack() as ctx:
+        pool = ctx.enter_context(tc.tile_pool(name="sbuf", bufs=1))
+        psum = ctx.enter_context(tc.psum_pool(name="psum", bufs=1))
+        ctx.enter_context(tc.manual_schedule())
+
+        q_rows = q.rearrange("(g c) (p j) n -> g (c p) j n", c=SIDE, j=PACK)
+        s_rows = S.rearrange("(g c) (p j) e -> g (c p) (j e)", c=SIDE, j=PACK)
+
+        weight = pool.tile([P, PACK], F32, name="weight")
+        qa_rows = qa.rearrange("(p j) o -> p (j o)", j=PACK)
+        nc.scalar.dma_start(out=weight[:], in_=qa_rows.partition_broadcast(SIDE))
+
+        raw = {}
+        s_raw = {}
+
+        def load_q(t, j0, count):
+            g, half = divmod(t, N // CHUNK)
+            piece = pool.tile([P, count, CHUNK], F32, name="raw_%d_%d" % (t, j0))
+            nc.sync.dma_start(out=piece[:], in_=q_rows[g, :, j0 : j0 + count, half * CHUNK : (half + 1) * CHUNK])
+            for j in range(count):
+                raw[t, j0 + j] = piece[:, j, :]
+
+        def load_s(g):
+            piece = pool.tile([P, PACK * E], F32, name="s_raw_%d" % g)
+            nc.sync.dma_start(out=piece[:], in_=s_rows[g])
+            s_raw[g] = piece
+
+        for j in range(PACK):
+            load_q(0, j, 1)
+        load_s(0)
+        load_q(1, 0, 2)
+        load_q(1, 2, 2)
+        load_s(1)
+        load_q(2, 0, 2)
+        load_q(2, 2, 2)
+        for j in range(PACK):
+            load_q(3, j, 1)
+
+        floor = pool.tile([P, PACK], F32, name="floor")
+        side = pool.tile([P, PACK], F32, name="side")
+        low = pool.tile([P, PACK], F32, name="low")
+        high = pool.tile([P, PACK], F32, name="high")
+        nc.vector.tensor_scalar(out=side[:], in0=weight[:], scalar1=0.0, scalar2=2.0 * FAR, op0=ALU.is_ge, op1=ALU.mult)
+        nc.vector.tensor_scalar(out=floor[:], in0=weight[:], scalar1=OFFSET, scalar2=None, op0=ALU.mult)
+        nc.vector.scalar_tensor_tensor(out=low[:], in0=side[:], scalar=FAR, in1=floor[:], op0=ALU.subtract, op1=ALU.min)
+        nc.vector.scalar_tensor_tensor(out=high[:], in0=side[:], scalar=FAR, in1=floor[:], op0=ALU.subtract, op1=ALU.max)
+
+        line = {}
+        mapped = [pool.tile([P, PACK, CHUNK], BF16, name="mapped_%d" % t) for t in range(CHUNKS)]
+        words = [pool.tile([P, CHUNK * PACK], BF16, name="words_%d" % t, align_bytes=64) for t in range(CHUNKS)]
+        codes = [pool.tile([P, CHUNK], U32, name="codes_%d" % t, align_bytes=64) for t in range(CHUNKS)]
+        scales = [pool.tile([P, CHUNK], U8, name="scales_%d" % t, align_bytes=64) for t in range(CHUNKS)]
+        s_words = [pool.tile([P, E * PACK], BF16, name="s_words_%d" % g, align_bytes=64) for g in range(PAIRS)]
+        s_codes = [pool.tile([P, E], U32, name="s_codes_%d" % g, align_bytes=64) for g in range(PAIRS)]
+        s_scales = [pool.tile([P, E], U8, name="s_scales_%d" % g, align_bytes=64) for g in range(PAIRS)]
+        sums = {(t, c): psum.tile([P, DEAL, E], F32, name="sums_%d_%d" % (t, c)) for t in range(CHUNKS) for c in range(SIDE)}
+        inverse = {(t, c): pool.tile([P, DEAL], F32, name="inverse_%d_%d" % (t, c)) for t in range(CHUNKS) for c in range(SIDE)}
+        result = {(t, c): pool.tile([P, DEAL, E], F32, name="result_%d_%d" % (t, c)) for t in range(CHUNKS) for c in range(SIDE)}
+
+        def line_scalar(t, j):
+            line[t, j] = pool.tile([P, CHUNK], BF16, name="line_%d_%d" % (t, j))
+            nc.scalar.activation(out=line[t, j][:], in_=raw[t, j], func=ACT.Identity, scale=weight[:, j : j + 1], bias=floor[:, j : j + 1])
+
+        def line_vector(t, j):
+            line[t, j] = pool.tile([P, CHUNK], BF16, name="line_%d_%d" % (t, j))
+            nc.vector.tensor_scalar(out=line[t, j][:], in0=raw[t, j], scalar1=OFFSET, scalar2=weight[:, j : j + 1], op0=ALU.add, op1=ALU.mult)
+
+        def clamp(t, j):
+            nc.vector.tensor_scalar(
+                out=mapped[t][:, j, :], in0=line[t, j][:], scalar1=low[:, j : j + 1], scalar2=high[:, j : j + 1], op0=ALU.max, op1=ALU.min
+            )
+
+        def interleave(t):
+            nc.vector.tensor_copy(
+                out=words[t][:].rearrange("p (r m j) -> p m j r", r=DEAL, j=PACK),
+                in_=mapped[t][:].rearrange("p j (m r) -> p m j r", r=DEAL),
+            )
+
+        def quantize(t):
+            nc.vector.quantize_mx(out=codes[t][:].bitcast(FP8X4), scales=scales[t][:], in_=words[t][:])
+
+        def interleave_s(g):
+            nc.scalar.copy(
+                out=s_words[g][:].rearrange("p (a i j) -> p a j i", i=4, j=PACK),
+                in_=s_raw[g][:].rearrange("p (j a i) -> p a j i", i=4, j=PACK),
+            )
+
+        def quantize_s(g):
+            nc.vector.quantize_mx(out=s_codes[g][:].bitcast(FP8X4), scales=s_scales[g][:], in_=s_words[g][:])
+
+        def multiply(t):
+            g = t // (N // CHUNK)
+            for r in range(DEAL):
+                for c in range(SIDE):
+                    rows = slice(c * ROWS, (c + 1) * ROWS)
+                    cols = slice(r * P, (r + 1) * P)
+                    nc.tensor.matmul_mx(
+                        out=sums[t, c][:, r, :],
+                        lhsT=codes[t][rows, cols].bitcast(FP8X4),
+                        lhsT_scale=scales[t][rows, cols],
+                        rhs=s_codes[g][rows, :].bitcast(FP8X4),
+                        rhs_scale=s_scales[g][rows, :],
+                        start=True,
+                        stop=True,
+                    )
+
+        def invert(t):
+            for c in range(SIDE):
+                nc.vector.reciprocal(out=inverse[t, c][:], in_=sums[t, c][:, :, E - 1])
+
+        def store(t, c):
+            g, half = divmod(t, N // CHUNK)
+            rows = out[g * SIDE + c, half * CHUNK : (half + 1) * CHUNK, :].rearrange("(m r) e -> m r e", r=DEAL)
+            nc.sync.dma_start(out=rows, in_=result[t, c][:])
+
+        def divide_scalar(t, c):
+            for r in range(DEAL):
+                nc.scalar.activation(out=result[t, c][:, r, :], in_=sums[t, c][:, r, :], func=ACT.Copy, scale=inverse[t, c][:, r : r + 1])
+            store(t, c)
+
+        def divide_vector(t, c):
+            nc.vector.tensor_tensor(
+                out=result[t, c][:], in0=sums[t, c][:], in1=inverse[t, c][:].unsqueeze(2).to_broadcast([P, DEAL, E]), op=ALU.mult
+            )
+            store(t, c)
+
+        line_scalar(0, 0)
+        line_vector(0, 1)
+        clamp(0, 0)
+        line_scalar(0, 2)
+        clamp(0, 1)
+        line_vector(0, 3)
+        clamp(0, 2)
+        clamp(0, 3)
+        interleave_s(0)
+        interleave(0)
+        quantize_s(0)
+        quantize(0)
+        multiply(0)
+
+        for j in range(3):
+            line_scalar(1, j)
+        clamp(1, 0)
+        clamp(1, 1)
+        line_vector(1, 3)
+        invert(0)
+        clamp(1, 3)
+        clamp(1, 2)
+        interleave_s(1)
+        divide_scalar(0, 0)
+        interleave(1)
+        quantize_s(1)
+        quantize(1)
+        multiply(1)
+
+        for j in range(3):
+            line_scalar(2, j)
+        clamp(2, 0)
+        clamp(2, 1)
+        line_vector(2, 3)
+        invert(1)
+        clamp(2, 3)
+        clamp(2, 2)
+        interleave(2)
+        for j in range(3):
+            line_scalar(3, j)
+        clamp(3, 0)
+        quantize(2)
+        multiply(2)
+        divide_scalar(0, 1)
+        divide_scalar(1, 0)
+        divide_scalar(1, 1)
+
+        line_vector(3, 3)
+        clamp(3, 1)
+        clamp(3, 2)
+        clamp(3, 3)
+        invert(2)
+        interleave(3)
+        divide_scalar(2, 0)
+        divide_scalar(2, 1)
+        quantize(3)
+        multiply(3)
+        invert(3)
+        divide_vector(3, 1)
+        divide_scalar(3, 0)

@@ -18,9 +18,8 @@ PACK = 4
 ROWS = D // PACK
 SIDE = P // ROWS
 PAIRS = H // SIDE
-CHUNK = 512
-DEAL = CHUNK // P
-CHUNKS = PAIRS * (N // CHUNK)
+BANKS = 4
+CHUNKS = [(0, 0, 512), (0, 512, 512), (1, 0, 512), (1, 512, 256), (1, 768, 256)]
 OFFSET = 0.125
 FAR = 1.5e38
 
@@ -37,15 +36,18 @@ def tile_rows_read_relu1_norm_kernel(tc, q, qa, S, out):
 
         weight = pool.tile([P, PACK], F32, name="weight")
         qa_rows = qa.rearrange("(p j) o -> p (j o)", j=PACK)
-        nc.scalar.dma_start(out=weight[:], in_=qa_rows.partition_broadcast(SIDE))
+
+        def load_qa():
+            for c in range(SIDE):
+                nc.sync.dma_start(out=weight[c * ROWS : (c + 1) * ROWS, :], in_=qa_rows)
 
         raw = {}
         s_raw = {}
 
         def load_q(t, j0, count):
-            g, half = divmod(t, N // CHUNK)
-            piece = pool.tile([P, count, CHUNK], F32, name="raw_%d_%d" % (t, j0))
-            nc.sync.dma_start(out=piece[:], in_=q_rows[g, :, j0 : j0 + count, half * CHUNK : (half + 1) * CHUNK])
+            g, n0, width = CHUNKS[t]
+            piece = pool.tile([P, count, width], F32, name="raw_%d_%d" % (t, j0))
+            nc.sync.dma_start(out=piece[:], in_=q_rows[g, :, j0 : j0 + count, n0 : n0 + width])
             for j in range(count):
                 raw[t, j0 + j] = piece[:, j, :]
 
@@ -54,44 +56,55 @@ def tile_rows_read_relu1_norm_kernel(tc, q, qa, S, out):
             nc.sync.dma_start(out=piece[:], in_=s_rows[g])
             s_raw[g] = piece
 
-        for j in range(PACK):
-            load_q(0, j, 1)
+        load_qa()
+        load_q(0, 0, 1)
+        load_q(0, 1, 1)
+        load_q(0, 2, 1)
+        load_q(0, 3, 1)
         load_s(0)
-        load_q(1, 0, 2)
-        load_q(1, 2, 2)
+        load_q(1, 0, 1)
+        load_q(1, 1, 1)
+        load_q(1, 2, 1)
+        load_q(1, 3, 1)
         load_s(1)
-        load_q(2, 0, 2)
-        load_q(2, 2, 2)
-        for j in range(PACK):
-            load_q(3, j, 1)
+        load_q(2, 0, 1)
+        load_q(2, 1, 1)
+        load_q(2, 2, 1)
+        load_q(2, 3, 1)
+        load_q(3, 0, 2)
+        load_q(3, 2, 2)
+        load_q(4, 0, 2)
+        load_q(4, 2, 2)
 
         floor = pool.tile([P, PACK], F32, name="floor")
         side = pool.tile([P, PACK], F32, name="side")
         low = pool.tile([P, PACK], F32, name="low")
         high = pool.tile([P, PACK], F32, name="high")
-        nc.vector.tensor_scalar(out=side[:], in0=weight[:], scalar1=0.0, scalar2=2.0 * FAR, op0=ALU.is_ge, op1=ALU.mult)
         nc.vector.tensor_scalar(out=floor[:], in0=weight[:], scalar1=OFFSET, scalar2=None, op0=ALU.mult)
+        nc.vector.tensor_scalar(out=side[:], in0=weight[:], scalar1=0.0, scalar2=2.0 * FAR, op0=ALU.is_ge, op1=ALU.mult)
         nc.vector.scalar_tensor_tensor(out=low[:], in0=side[:], scalar=FAR, in1=floor[:], op0=ALU.subtract, op1=ALU.min)
         nc.vector.scalar_tensor_tensor(out=high[:], in0=side[:], scalar=FAR, in1=floor[:], op0=ALU.subtract, op1=ALU.max)
 
+        count = len(CHUNKS)
+        widths = [width for g, n0, width in CHUNKS]
         line = {}
-        mapped = [pool.tile([P, PACK, CHUNK], BF16, name="mapped_%d" % t) for t in range(CHUNKS)]
-        words = [pool.tile([P, CHUNK * PACK], BF16, name="words_%d" % t, align_bytes=64) for t in range(CHUNKS)]
-        codes = [pool.tile([P, CHUNK], U32, name="codes_%d" % t, align_bytes=64) for t in range(CHUNKS)]
-        scales = [pool.tile([P, CHUNK], U8, name="scales_%d" % t, align_bytes=64) for t in range(CHUNKS)]
+        sums = {}
+        mapped = [pool.tile([P, PACK, widths[t]], BF16, name="mapped_%d" % t) for t in range(count)]
+        words = [pool.tile([P, widths[t] * PACK], BF16, name="words_%d" % t, align_bytes=64) for t in range(count)]
+        codes = [pool.tile([P, widths[t]], U32, name="codes_%d" % t, align_bytes=64) for t in range(count)]
+        scales = [pool.tile([P, widths[t]], U8, name="scales_%d" % t, align_bytes=64) for t in range(count)]
         s_words = [pool.tile([P, E * PACK], BF16, name="s_words_%d" % g, align_bytes=64) for g in range(PAIRS)]
         s_codes = [pool.tile([P, E], U32, name="s_codes_%d" % g, align_bytes=64) for g in range(PAIRS)]
         s_scales = [pool.tile([P, E], U8, name="s_scales_%d" % g, align_bytes=64) for g in range(PAIRS)]
-        sums = {(t, c): psum.tile([P, DEAL, E], F32, name="sums_%d_%d" % (t, c)) for t in range(CHUNKS) for c in range(SIDE)}
-        inverse = {(t, c): pool.tile([P, DEAL], F32, name="inverse_%d_%d" % (t, c)) for t in range(CHUNKS) for c in range(SIDE)}
-        result = {(t, c): pool.tile([P, DEAL, E], F32, name="result_%d_%d" % (t, c)) for t in range(CHUNKS) for c in range(SIDE)}
+        inverse = {(t, c): pool.tile([P, widths[t] // P], F32, name="inverse_%d_%d" % (t, c)) for t in range(count) for c in range(SIDE)}
+        result = {(t, c): pool.tile([P, widths[t] // P, E], F32, name="result_%d_%d" % (t, c)) for t in range(count) for c in range(SIDE)}
 
         def line_scalar(t, j):
-            line[t, j] = pool.tile([P, CHUNK], BF16, name="line_%d_%d" % (t, j))
+            line[t, j] = pool.tile([P, widths[t]], BF16, name="line_%d_%d" % (t, j))
             nc.scalar.activation(out=line[t, j][:], in_=raw[t, j], func=ACT.Identity, scale=weight[:, j : j + 1], bias=floor[:, j : j + 1])
 
         def line_vector(t, j):
-            line[t, j] = pool.tile([P, CHUNK], BF16, name="line_%d_%d" % (t, j))
+            line[t, j] = pool.tile([P, widths[t]], BF16, name="line_%d_%d" % (t, j))
             nc.vector.tensor_scalar(out=line[t, j][:], in0=raw[t, j], scalar1=OFFSET, scalar2=weight[:, j : j + 1], op0=ALU.add, op1=ALU.mult)
 
         def clamp(t, j):
@@ -101,8 +114,8 @@ def tile_rows_read_relu1_norm_kernel(tc, q, qa, S, out):
 
         def interleave(t):
             nc.vector.tensor_copy(
-                out=words[t][:].rearrange("p (r m j) -> p m j r", r=DEAL, j=PACK),
-                in_=mapped[t][:].rearrange("p j (m r) -> p m j r", r=DEAL),
+                out=words[t][:].rearrange("p (r m j) -> p r m j", m=P, j=PACK),
+                in_=mapped[t][:].rearrange("p j (m r) -> p r m j", m=P),
             )
 
         def quantize(t):
@@ -114,12 +127,20 @@ def tile_rows_read_relu1_norm_kernel(tc, q, qa, S, out):
                 in_=s_raw[g][:].rearrange("p (j a i) -> p a j i", i=4, j=PACK),
             )
 
+        def interleave_s_vector(g):
+            nc.vector.tensor_copy(
+                out=s_words[g][:].rearrange("p (a i j) -> p a j i", i=4, j=PACK),
+                in_=s_raw[g][:].rearrange("p (j a i) -> p a j i", i=4, j=PACK),
+            )
+
         def quantize_s(g):
             nc.vector.quantize_mx(out=s_codes[g][:].bitcast(FP8X4), scales=s_scales[g][:], in_=s_words[g][:])
 
         def multiply(t):
-            g = t // (N // CHUNK)
-            for r in range(DEAL):
+            g = CHUNKS[t][0]
+            for c in range(SIDE):
+                sums[t, c] = psum.tile([P, BANKS, E], F32, name="sums_%d_%d" % (t, c), tag="bank_%d_%d" % (t % BANKS, c))
+            for r in range(widths[t] // P):
                 for c in range(SIDE):
                     rows = slice(c * ROWS, (c + 1) * ROWS)
                     cols = slice(r * P, (r + 1) * P)
@@ -133,23 +154,23 @@ def tile_rows_read_relu1_norm_kernel(tc, q, qa, S, out):
                         stop=True,
                     )
 
-        def invert(t):
-            for c in range(SIDE):
-                nc.vector.reciprocal(out=inverse[t, c][:], in_=sums[t, c][:, :, E - 1])
+        def invert(t, c):
+            nc.vector.reciprocal(out=inverse[t, c][:], in_=sums[t, c][:, 0 : widths[t] // P, E - 1])
 
         def store(t, c):
-            g, half = divmod(t, N // CHUNK)
-            rows = out[g * SIDE + c, half * CHUNK : (half + 1) * CHUNK, :].rearrange("(m r) e -> m r e", r=DEAL)
+            g, n0, width = CHUNKS[t]
+            rows = out[g * SIDE + c, n0 : n0 + width, :].rearrange("(m r) e -> m r e", m=P)
             nc.sync.dma_start(out=rows, in_=result[t, c][:])
 
         def divide_scalar(t, c):
-            for r in range(DEAL):
+            for r in range(widths[t] // P):
                 nc.scalar.activation(out=result[t, c][:, r, :], in_=sums[t, c][:, r, :], func=ACT.Copy, scale=inverse[t, c][:, r : r + 1])
             store(t, c)
 
         def divide_vector(t, c):
+            deal = widths[t] // P
             nc.vector.tensor_tensor(
-                out=result[t, c][:], in0=sums[t, c][:], in1=inverse[t, c][:].unsqueeze(2).to_broadcast([P, DEAL, E]), op=ALU.mult
+                out=result[t, c][:], in0=sums[t, c][:, 0:deal, :], in1=inverse[t, c][:].unsqueeze(2).to_broadcast([P, deal, E]), op=ALU.mult
             )
             store(t, c)
 
@@ -163,53 +184,72 @@ def tile_rows_read_relu1_norm_kernel(tc, q, qa, S, out):
         clamp(0, 3)
         interleave_s(0)
         interleave(0)
+        line_scalar(1, 0)
+        line_scalar(1, 1)
+        line_scalar(1, 2)
+        line_scalar(1, 3)
         quantize_s(0)
+        clamp(1, 0)
         quantize(0)
         multiply(0)
-
-        for j in range(3):
-            line_scalar(1, j)
-        clamp(1, 0)
         clamp(1, 1)
-        line_vector(1, 3)
-        invert(0)
-        clamp(1, 3)
         clamp(1, 2)
+        clamp(1, 3)
         interleave_s(1)
-        divide_scalar(0, 0)
+        line_scalar(2, 0)
+        line_scalar(2, 1)
+        line_scalar(2, 2)
+        line_scalar(2, 3)
         interleave(1)
         quantize_s(1)
+        invert(0, 0)
+        invert(0, 1)
+        clamp(2, 0)
         quantize(1)
         multiply(1)
-
-        for j in range(3):
-            line_scalar(2, j)
-        clamp(2, 0)
         clamp(2, 1)
-        line_vector(2, 3)
-        invert(1)
-        clamp(2, 3)
         clamp(2, 2)
+        clamp(2, 3)
+        divide_scalar(0, 0)
+        line_scalar(3, 0)
+        line_scalar(3, 1)
+        line_scalar(3, 2)
+        line_scalar(3, 3)
         interleave(2)
-        for j in range(3):
-            line_scalar(3, j)
+        line_scalar(4, 0)
+        line_scalar(4, 1)
+        line_scalar(4, 2)
+        line_scalar(4, 3)
+        divide_scalar(0, 1)
+        invert(1, 0)
+        invert(1, 1)
         clamp(3, 0)
+        clamp(3, 1)
         quantize(2)
         multiply(2)
-        divide_scalar(0, 1)
-        divide_scalar(1, 0)
-        divide_scalar(1, 1)
-
-        line_vector(3, 3)
-        clamp(3, 1)
         clamp(3, 2)
         clamp(3, 3)
-        invert(2)
+        clamp(4, 0)
+        clamp(4, 1)
+        clamp(4, 2)
+        clamp(4, 3)
+        divide_scalar(1, 0)
+        divide_scalar(1, 1)
         interleave(3)
-        divide_scalar(2, 0)
-        divide_scalar(2, 1)
+        interleave(4)
+        invert(2, 0)
+        invert(2, 1)
         quantize(3)
         multiply(3)
-        invert(3)
-        divide_vector(3, 1)
+        quantize(4)
+        multiply(4)
+        divide_scalar(2, 0)
+        divide_vector(2, 1)
+        invert(3, 0)
+        invert(3, 1)
+        invert(4, 0)
+        invert(4, 1)
         divide_scalar(3, 0)
+        divide_vector(3, 1)
+        divide_scalar(4, 0)
+        divide_vector(4, 1)

@@ -114,8 +114,8 @@ def tile_rows_read_relu1_norm_kernel(tc, q, qa, S, out):
 
         def interleave(t):
             nc.vector.tensor_copy(
-                out=words[t][:].rearrange("p (r m j) -> p r m j", m=P, j=PACK),
-                in_=mapped[t][:].rearrange("p j (m r) -> p r m j", m=P),
+                out=words[t][:].rearrange("p (r m j) -> p m j r", m=P, j=PACK),
+                in_=mapped[t][:].rearrange("p j (m r) -> p m j r", m=P),
             )
 
         def quantize(t):

@@ -19,13 +19,19 @@ ROWS = D // PACK
 SIDE = P // ROWS
 PAIRS = H // SIDE
 BANKS = 4
-CHUNKS = [(0, 0, 512), (0, 512, 512), (1, 0, 512), (1, 512, 256), (1, 768, 256)]
+BANK_SUMS = 4
+RUN = 4
 OFFSET = 0.125
 FAR = 1.5e38
+
+CHUNKS = [(0, 0, 512), (0, 512, 512), (1, 0, 512), (1, 512, 256), (1, 768, 256)]
+WIDE = 512
 
 
 def tile_rows_read_relu1_norm_kernel(tc, q, qa, S, out):
     nc = tc.nc
+    count = len(CHUNKS)
+    widths = [width for g, n0, width in CHUNKS]
     with ExitStack() as ctx:
         pool = ctx.enter_context(tc.tile_pool(name="sbuf", bufs=1))
         psum = ctx.enter_context(tc.psum_pool(name="psum", bufs=1))
@@ -33,77 +39,50 @@ def tile_rows_read_relu1_norm_kernel(tc, q, qa, S, out):
 
         q_rows = q.rearrange("(g c) (p j) n -> g (c p) j n", c=SIDE, j=PACK)
         s_rows = S.rearrange("(g c) (p j) e -> g (c p) (j e)", c=SIDE, j=PACK)
-
-        weight = pool.tile([P, PACK], F32, name="weight")
         qa_rows = qa.rearrange("(p j) o -> p (j o)", j=PACK)
-
-        def load_qa():
-            for c in range(SIDE):
-                nc.sync.dma_start(out=weight[c * ROWS : (c + 1) * ROWS, :], in_=qa_rows)
+        weight = pool.tile([P, PACK], F32, name="weight")
+        for c in range(SIDE):
+            nc.sync.dma_start(out=weight[c * ROWS : (c + 1) * ROWS, :], in_=qa_rows)
 
         raw = {}
         s_raw = {}
+        for t, (g, n0, width) in enumerate(CHUNKS):
+            per_piece = WIDE // width
+            for j0 in range(0, PACK, per_piece):
+                piece = pool.tile([P, per_piece, width], F32, name="raw_%d_%d" % (t, j0))
+                nc.sync.dma_start(out=piece[:], in_=q_rows[g, :, j0 : j0 + per_piece, n0 : n0 + width])
+                for j in range(per_piece):
+                    raw[t, j0 + j] = piece[:, j, :]
+            if n0 == 0:
+                s_raw[g] = pool.tile([P, PACK * E], F32, name="s_raw_%d" % g)
+                nc.sync.dma_start(out=s_raw[g][:], in_=s_rows[g])
 
-        def load_q(t, j0, count):
-            g, n0, width = CHUNKS[t]
-            piece = pool.tile([P, count, width], F32, name="raw_%d_%d" % (t, j0))
-            nc.sync.dma_start(out=piece[:], in_=q_rows[g, :, j0 : j0 + count, n0 : n0 + width])
-            for j in range(count):
-                raw[t, j0 + j] = piece[:, j, :]
-
-        def load_s(g):
-            piece = pool.tile([P, PACK * E], F32, name="s_raw_%d" % g)
-            nc.sync.dma_start(out=piece[:], in_=s_rows[g])
-            s_raw[g] = piece
-
-        load_qa()
-        load_q(0, 0, 1)
-        load_q(0, 1, 1)
-        load_q(0, 2, 1)
-        load_q(0, 3, 1)
-        load_s(0)
-        load_q(1, 0, 1)
-        load_q(1, 1, 1)
-        load_q(1, 2, 1)
-        load_q(1, 3, 1)
-        load_s(1)
-        load_q(2, 0, 1)
-        load_q(2, 1, 1)
-        load_q(2, 2, 1)
-        load_q(2, 3, 1)
-        load_q(3, 0, 2)
-        load_q(3, 2, 2)
-        load_q(4, 0, 2)
-        load_q(4, 2, 2)
-
-        floor = pool.tile([P, PACK], F32, name="floor")
-        side = pool.tile([P, PACK], F32, name="side")
+        level = pool.tile([P, PACK], F32, name="level")
+        sign_step = pool.tile([P, PACK], F32, name="sign_step")
         low = pool.tile([P, PACK], F32, name="low")
         high = pool.tile([P, PACK], F32, name="high")
-        nc.vector.tensor_scalar(out=floor[:], in0=weight[:], scalar1=OFFSET, scalar2=None, op0=ALU.mult)
-        nc.vector.tensor_scalar(out=side[:], in0=weight[:], scalar1=0.0, scalar2=2.0 * FAR, op0=ALU.is_ge, op1=ALU.mult)
-        nc.vector.scalar_tensor_tensor(out=low[:], in0=side[:], scalar=FAR, in1=floor[:], op0=ALU.subtract, op1=ALU.min)
-        nc.vector.scalar_tensor_tensor(out=high[:], in0=side[:], scalar=FAR, in1=floor[:], op0=ALU.subtract, op1=ALU.max)
+        nc.vector.tensor_scalar(out=level[:], in0=weight[:], scalar1=OFFSET, scalar2=None, op0=ALU.mult)
+        nc.vector.tensor_scalar(out=sign_step[:], in0=weight[:], scalar1=0.0, scalar2=2.0 * FAR, op0=ALU.is_ge, op1=ALU.mult)
+        nc.vector.scalar_tensor_tensor(out=low[:], in0=sign_step[:], scalar=FAR, in1=level[:], op0=ALU.subtract, op1=ALU.min)
+        nc.vector.scalar_tensor_tensor(out=high[:], in0=sign_step[:], scalar=FAR, in1=level[:], op0=ALU.subtract, op1=ALU.max)
 
-        count = len(CHUNKS)
-        widths = [width for g, n0, width in CHUNKS]
         line = {}
         sums = {}
         mapped = [pool.tile([P, PACK, widths[t]], BF16, name="mapped_%d" % t) for t in range(count)]
-        words = [pool.tile([P, widths[t] * PACK], BF16, name="words_%d" % t, align_bytes=64) for t in range(count)]
+        grouped = [pool.tile([P, widths[t] * PACK], BF16, name="grouped_%d" % t, align_bytes=64) for t in range(count)]
         codes = [pool.tile([P, widths[t]], U32, name="codes_%d" % t, align_bytes=64) for t in range(count)]
         scales = [pool.tile([P, widths[t]], U8, name="scales_%d" % t, align_bytes=64) for t in range(count)]
-        s_words = [pool.tile([P, E * PACK], BF16, name="s_words_%d" % g, align_bytes=64) for g in range(PAIRS)]
+        s_grouped = [pool.tile([P, E * PACK], BF16, name="s_grouped_%d" % g, align_bytes=64) for g in range(PAIRS)]
         s_codes = [pool.tile([P, E], U32, name="s_codes_%d" % g, align_bytes=64) for g in range(PAIRS)]
         s_scales = [pool.tile([P, E], U8, name="s_scales_%d" % g, align_bytes=64) for g in range(PAIRS)]
         inverse = {(t, c): pool.tile([P, widths[t] // P], F32, name="inverse_%d_%d" % (t, c)) for t in range(count) for c in range(SIDE)}
         result = {(t, c): pool.tile([P, widths[t] // P, E], F32, name="result_%d_%d" % (t, c)) for t in range(count) for c in range(SIDE)}
 
-        def line_scalar(t, j):
+        def line_on_scalar(t, j):
             line[t, j] = pool.tile([P, widths[t]], BF16, name="line_%d_%d" % (t, j))
-            nc.scalar.activation(out=line[t, j][:], in_=raw[t, j], func=ACT.Identity, scale=weight[:, j : j + 1], bias=floor[:, j : j + 1])
+            nc.scalar.activation(out=line[t, j][:], in_=raw[t, j], func=ACT.Identity, scale=weight[:, j : j + 1], bias=level[:, j : j + 1])
 
-        def line_vector(t, j):
+        def line_on_vector(t, j):
             line[t, j] = pool.tile([P, widths[t]], BF16, name="line_%d_%d" % (t, j))
             nc.vector.tensor_scalar(out=line[t, j][:], in0=raw[t, j], scalar1=OFFSET, scalar2=weight[:, j : j + 1], op0=ALU.add, op1=ALU.mult)
 
@@ -113,33 +92,28 @@ def tile_rows_read_relu1_norm_kernel(tc, q, qa, S, out):
             )
 
         def interleave(t):
+            along = RUN * P // widths[t]
             nc.vector.tensor_copy(
-                out=words[t][:].rearrange("p (r m j) -> p m j r", m=P, j=PACK),
-                in_=mapped[t][:].rearrange("p j (m r) -> p m j r", m=P),
+                out=grouped[t][:].rearrange("p (r a b j) -> p a j b r", a=P // along, b=along, j=PACK),
+                in_=mapped[t][:].rearrange("p j (a b r) -> p a j b r", a=P // along, b=along),
             )
 
         def quantize(t):
-            nc.vector.quantize_mx(out=codes[t][:].bitcast(FP8X4), scales=scales[t][:], in_=words[t][:])
+            nc.vector.quantize_mx(out=codes[t][:].bitcast(FP8X4), scales=scales[t][:], in_=grouped[t][:])
 
-        def interleave_s(g):
+        def interleave_state(g):
             nc.scalar.copy(
-                out=s_words[g][:].rearrange("p (a i j) -> p a j i", i=4, j=PACK),
-                in_=s_raw[g][:].rearrange("p (j a i) -> p a j i", i=4, j=PACK),
+                out=s_grouped[g][:].rearrange("p (a b j) -> p a j b", b=RUN, j=PACK),
+                in_=s_raw[g][:].rearrange("p (j a b) -> p a j b", b=RUN, j=PACK),
             )
 
-        def interleave_s_vector(g):
-            nc.vector.tensor_copy(
-                out=s_words[g][:].rearrange("p (a i j) -> p a j i", i=4, j=PACK),
-                in_=s_raw[g][:].rearrange("p (j a i) -> p a j i", i=4, j=PACK),
-            )
-
-        def quantize_s(g):
-            nc.vector.quantize_mx(out=s_codes[g][:].bitcast(FP8X4), scales=s_scales[g][:], in_=s_words[g][:])
+        def quantize_state(g):
+            nc.vector.quantize_mx(out=s_codes[g][:].bitcast(FP8X4), scales=s_scales[g][:], in_=s_grouped[g][:])
 
         def multiply(t):
             g = CHUNKS[t][0]
             for c in range(SIDE):
-                sums[t, c] = psum.tile([P, BANKS, E], F32, name="sums_%d_%d" % (t, c), tag="bank_%d_%d" % (t % BANKS, c))
+                sums[t, c] = psum.tile([P, BANK_SUMS, E], F32, name="sums_%d_%d" % (t, c), tag="bank_%d_%d" % (t % BANKS, c))
             for r in range(widths[t] // P):
                 for c in range(SIDE):
                     rows = slice(c * ROWS, (c + 1) * ROWS)
@@ -154,102 +128,73 @@ def tile_rows_read_relu1_norm_kernel(tc, q, qa, S, out):
                         stop=True,
                     )
 
-        def invert(t, c):
-            nc.vector.reciprocal(out=inverse[t, c][:], in_=sums[t, c][:, 0 : widths[t] // P, E - 1])
+        def invert(t):
+            for c in range(SIDE):
+                nc.vector.reciprocal(out=inverse[t, c][:], in_=sums[t, c][:, 0 : widths[t] // P, E - 1])
 
         def store(t, c):
             g, n0, width = CHUNKS[t]
-            rows = out[g * SIDE + c, n0 : n0 + width, :].rearrange("(m r) e -> m r e", m=P)
-            nc.sync.dma_start(out=rows, in_=result[t, c][:])
+            rows_out = out[g * SIDE + c, n0 : n0 + width, :].rearrange("(m r) e -> m r e", m=P)
+            nc.sync.dma_start(out=rows_out, in_=result[t, c][:])
 
-        def divide_scalar(t, c):
+        def divide_on_scalar(t, c):
             for r in range(widths[t] // P):
                 nc.scalar.activation(out=result[t, c][:, r, :], in_=sums[t, c][:, r, :], func=ACT.Copy, scale=inverse[t, c][:, r : r + 1])
             store(t, c)
 
-        def divide_vector(t, c):
+        def divide_on_vector(t, c):
             deal = widths[t] // P
             nc.vector.tensor_tensor(
                 out=result[t, c][:], in0=sums[t, c][:, 0:deal, :], in1=inverse[t, c][:].unsqueeze(2).to_broadcast([P, deal, E]), op=ALU.mult
             )
             store(t, c)
 
-        line_scalar(0, 0)
-        line_vector(0, 1)
+        line_on_scalar(0, 0)
+        line_on_vector(0, 1)
         clamp(0, 0)
-        line_scalar(0, 2)
+        line_on_scalar(0, 2)
         clamp(0, 1)
-        line_vector(0, 3)
+        line_on_vector(0, 3)
         clamp(0, 2)
         clamp(0, 3)
-        interleave_s(0)
-        interleave(0)
-        line_scalar(1, 0)
-        line_scalar(1, 1)
-        line_scalar(1, 2)
-        line_scalar(1, 3)
-        quantize_s(0)
-        clamp(1, 0)
-        quantize(0)
-        multiply(0)
-        clamp(1, 1)
-        clamp(1, 2)
-        clamp(1, 3)
-        interleave_s(1)
-        line_scalar(2, 0)
-        line_scalar(2, 1)
-        line_scalar(2, 2)
-        line_scalar(2, 3)
-        interleave(1)
-        quantize_s(1)
-        invert(0, 0)
-        invert(0, 1)
-        clamp(2, 0)
-        quantize(1)
-        multiply(1)
-        clamp(2, 1)
-        clamp(2, 2)
-        clamp(2, 3)
-        divide_scalar(0, 0)
-        line_scalar(3, 0)
-        line_scalar(3, 1)
-        line_scalar(3, 2)
-        line_scalar(3, 3)
-        interleave(2)
-        line_scalar(4, 0)
-        line_scalar(4, 1)
-        line_scalar(4, 2)
-        line_scalar(4, 3)
-        divide_scalar(0, 1)
-        invert(1, 0)
-        invert(1, 1)
-        clamp(3, 0)
-        clamp(3, 1)
-        quantize(2)
-        multiply(2)
-        clamp(3, 2)
-        clamp(3, 3)
-        clamp(4, 0)
-        clamp(4, 1)
-        clamp(4, 2)
-        clamp(4, 3)
-        divide_scalar(1, 0)
-        divide_scalar(1, 1)
-        interleave(3)
+        interleave_state(0)
+
+        for t in (0, 1):
+            for j in range(PACK):
+                line_on_scalar(t + 1, j)
+            interleave(t)
+            clamp(t + 1, 0)
+            if t == 0:
+                quantize_state(0)
+            else:
+                invert(t - 1)
+            quantize(t)
+            multiply(t)
+            for j in range(1, PACK):
+                clamp(t + 1, j)
+        interleave_state(1)
+
+        for t in (2, 3):
+            divide_on_scalar(0, t - 2)
+            line_on_vector(t + 1, 0)
+            for j in range(1, PACK):
+                line_on_scalar(t + 1, j)
+            if t == 2:
+                quantize_state(1)
+            interleave(t)
+            for j in range(PACK):
+                clamp(t + 1, j)
+            quantize(t)
+            multiply(t)
+            invert(t - 1)
+
+        for t in (1, 2):
+            for c in range(SIDE):
+                divide_on_scalar(t, c)
         interleave(4)
-        invert(2, 0)
-        invert(2, 1)
-        quantize(3)
-        multiply(3)
         quantize(4)
         multiply(4)
-        divide_scalar(2, 0)
-        divide_vector(2, 1)
-        invert(3, 0)
-        invert(3, 1)
-        invert(4, 0)
-        invert(4, 1)
-        divide_scalar(3, 0)
-        divide_vector(3, 1)
-        divide_scalar(4, 0)
-        divide_vector(4, 1)
+        for t in (3, 4):
+            invert(t)
+            divide_on_vector(t, 0)
+            divide_on_scalar(t, 1)

@@ -20,7 +20,9 @@ SIDE = P // ROWS
 PAIRS = H // SIDE
 BANKS = 4
 BANK_SUMS = 4
-RUN = 4
+LINE_BYTES = 16
+RUN_BF16 = LINE_BYTES // 2
+RUN_F32 = LINE_BYTES // 4
 OFFSET = 0.125
 FAR = 1.5e38
 
@@ -41,8 +43,6 @@ def tile_rows_read_relu1_norm_kernel(tc, q, qa, S, out):
         s_rows = S.rearrange("(g c) (p j) e -> g (c p) (j e)", c=SIDE, j=PACK)
         qa_rows = qa.rearrange("(p j) o -> p (j o)", j=PACK)
         weight = pool.tile([P, PACK], F32, name="weight")
-        for c in range(SIDE):
-            nc.sync.dma_start(out=weight[c * ROWS : (c + 1) * ROWS, :], in_=qa_rows)
 
         raw = {}
         s_raw = {}
@@ -53,6 +53,9 @@ def tile_rows_read_relu1_norm_kernel(tc, q, qa, S, out):
                 nc.sync.dma_start(out=piece[:], in_=q_rows[g, :, j0 : j0 + per_piece, n0 : n0 + width])
                 for j in range(per_piece):
                     raw[t, j0 + j] = piece[:, j, :]
+                if (t, j0) == (0, 0):
+                    for c in range(SIDE):
+                        nc.sync.dma_start(out=weight[c * ROWS : (c + 1) * ROWS, :], in_=qa_rows)
             if n0 == 0:
                 s_raw[g] = pool.tile([P, PACK * E], F32, name="s_raw_%d" % g)
                 nc.sync.dma_start(out=s_raw[g][:], in_=s_rows[g])
@@ -92,7 +95,7 @@ def tile_rows_read_relu1_norm_kernel(tc, q, qa, S, out):
             )
 
         def interleave(t):
-            along = RUN * P // widths[t]
+            along = RUN_BF16 * P // widths[t]
             nc.vector.tensor_copy(
                 out=grouped[t][:].rearrange("p (r a b j) -> p a j b r", a=P // along, b=along, j=PACK),
                 in_=mapped[t][:].rearrange("p j (a b r) -> p a j b r", a=P // along, b=along),
@@ -103,8 +106,8 @@ def tile_rows_read_relu1_norm_kernel(tc, q, qa, S, out):
 
         def interleave_state(g):
             nc.scalar.copy(
-                out=s_grouped[g][:].rearrange("p (a b j) -> p a j b", b=RUN, j=PACK),
-                in_=s_raw[g][:].rearrange("p (j a b) -> p a j b", b=RUN, j=PACK),
+                out=s_grouped[g][:].rearrange("p (a b j) -> p a j b", b=RUN_F32, j=PACK),
+                in_=s_raw[g][:].rearrange("p (j a b) -> p a j b", b=RUN_F32, j=PACK),
             )
 
         def quantize_state(g):

from contextlib import ExitStack

import concourse.mybir as mybir

H, D, N, E = 4, 256, 1024, 128
FLOPS = 2 * H * N * D * E

F32 = mybir.dt.float32
BF16 = mybir.dt.bfloat16
U32 = mybir.dt.uint32
U8 = mybir.dt.uint8
FP8X4 = mybir.dt.float8_e4m3fn_x4
ALU = mybir.AluOpType
ACT = mybir.ActivationFunctionType

P = 128
PACK = 4
ROWS = D // PACK
SIDE = P // ROWS
PAIRS = H // SIDE
BANKS = 4
BANK_SUMS = 4
LINE_BYTES = 16
RUN_BF16 = LINE_BYTES // 2
RUN_F32 = LINE_BYTES // 4
OFFSET = 0.125
FAR = 1.5e38

CHUNKS = [(0, 0, 512), (0, 512, 512), (1, 0, 512), (1, 512, 256), (1, 768, 256)]
WIDE = 512


def tile_rows_read_relu1_norm_kernel(tc, q, qa, S, out):
    nc = tc.nc
    count = len(CHUNKS)
    widths = [width for g, n0, width in CHUNKS]
    with ExitStack() as ctx:
        pool = ctx.enter_context(tc.tile_pool(name="sbuf", bufs=1))
        psum = ctx.enter_context(tc.psum_pool(name="psum", bufs=1))
        ctx.enter_context(tc.manual_schedule())

        q_rows = q.rearrange("(g c) (p j) n -> g (c p) j n", c=SIDE, j=PACK)
        s_rows = S.rearrange("(g c) (p j) e -> g (c p) (j e)", c=SIDE, j=PACK)
        qa_rows = qa.rearrange("(p j) o -> p (j o)", j=PACK)
        weight = pool.tile([P, PACK], F32, name="weight")

        raw = {}
        s_raw = {}
        for t, (g, n0, width) in enumerate(CHUNKS):
            per_piece = WIDE // width
            for j0 in range(0, PACK, per_piece):
                piece = pool.tile([P, per_piece, width], F32, name="raw_%d_%d" % (t, j0))
                nc.sync.dma_start(out=piece[:], in_=q_rows[g, :, j0 : j0 + per_piece, n0 : n0 + width])
                for j in range(per_piece):
                    raw[t, j0 + j] = piece[:, j, :]
                if (t, j0) == (0, 0):
                    for c in range(SIDE):
                        nc.sync.dma_start(out=weight[c * ROWS : (c + 1) * ROWS, :], in_=qa_rows)
            if n0 == 0:
                s_raw[g] = pool.tile([P, PACK * E], F32, name="s_raw_%d" % g)
                nc.sync.dma_start(out=s_raw[g][:], in_=s_rows[g])

        level = pool.tile([P, PACK], F32, name="level")
        sign_step = pool.tile([P, PACK], F32, name="sign_step")
        low = pool.tile([P, PACK], F32, name="low")
        high = pool.tile([P, PACK], F32, name="high")
        nc.vector.tensor_scalar(out=level[:], in0=weight[:], scalar1=OFFSET, scalar2=None, op0=ALU.mult)
        nc.vector.tensor_scalar(out=sign_step[:], in0=weight[:], scalar1=0.0, scalar2=2.0 * FAR, op0=ALU.is_ge, op1=ALU.mult)
        nc.vector.scalar_tensor_tensor(out=low[:], in0=sign_step[:], scalar=FAR, in1=level[:], op0=ALU.subtract, op1=ALU.min)
        nc.vector.scalar_tensor_tensor(out=high[:], in0=sign_step[:], scalar=FAR, in1=level[:], op0=ALU.subtract, op1=ALU.max)

        line = {}
        sums = {}
        mapped = [pool.tile([P, PACK, widths[t]], BF16, name="mapped_%d" % t) for t in range(count)]
        grouped = [pool.tile([P, widths[t] * PACK], BF16, name="grouped_%d" % t, align_bytes=64) for t in range(count)]
        codes = [pool.tile([P, widths[t]], U32, name="codes_%d" % t, align_bytes=64) for t in range(count)]
        scales = [pool.tile([P, widths[t]], U8, name="scales_%d" % t, align_bytes=64) for t in range(count)]
        s_grouped = [pool.tile([P, E * PACK], BF16, name="s_grouped_%d" % g, align_bytes=64) for g in range(PAIRS)]
        s_codes = [pool.tile([P, E], U32, name="s_codes_%d" % g, align_bytes=64) for g in range(PAIRS)]
        s_scales = [pool.tile([P, E], U8, name="s_scales_%d" % g, align_bytes=64) for g in range(PAIRS)]
        inverse = {(t, c): pool.tile([P, widths[t] // P], F32, name="inverse_%d_%d" % (t, c)) for t in range(count) for c in range(SIDE)}
        result = {(t, c): pool.tile([P, widths[t] // P, E], F32, name="result_%d_%d" % (t, c)) for t in range(count) for c in range(SIDE)}

        def line_on_scalar(t, j):
            line[t, j] = pool.tile([P, widths[t]], BF16, name="line_%d_%d" % (t, j))
            nc.scalar.activation(out=line[t, j][:], in_=raw[t, j], func=ACT.Identity, scale=weight[:, j : j + 1], bias=level[:, j : j + 1])

        def line_on_vector(t, j):
            line[t, j] = pool.tile([P, widths[t]], BF16, name="line_%d_%d" % (t, j))
            nc.vector.tensor_scalar(out=line[t, j][:], in0=raw[t, j], scalar1=OFFSET, scalar2=weight[:, j : j + 1], op0=ALU.add, op1=ALU.mult)

        def clamp(t, j):
            nc.vector.tensor_scalar(
                out=mapped[t][:, j, :], in0=line[t, j][:], scalar1=low[:, j : j + 1], scalar2=high[:, j : j + 1], op0=ALU.max, op1=ALU.min
            )

        def interleave(t):
            along = RUN_BF16 * P // widths[t]
            nc.vector.tensor_copy(
                out=grouped[t][:].rearrange("p (r a b j) -> p a j b r", a=P // along, b=along, j=PACK),
                in_=mapped[t][:].rearrange("p j (a b r) -> p a j b r", a=P // along, b=along),
            )

        def quantize(t):
            nc.vector.quantize_mx(out=codes[t][:].bitcast(FP8X4), scales=scales[t][:], in_=grouped[t][:])

        def interleave_state(g):
            nc.scalar.copy(
                out=s_grouped[g][:].rearrange("p (a b j) -> p a j b", b=RUN_F32, j=PACK),
                in_=s_raw[g][:].rearrange("p (j a b) -> p a j b", b=RUN_F32, j=PACK),
            )

        def quantize_state(g):
            nc.vector.quantize_mx(out=s_codes[g][:].bitcast(FP8X4), scales=s_scales[g][:], in_=s_grouped[g][:])

        def multiply(t):
            g = CHUNKS[t][0]
            for c in range(SIDE):
                sums[t, c] = psum.tile([P, BANK_SUMS, E], F32, name="sums_%d_%d" % (t, c), tag="bank_%d_%d" % (t % BANKS, c))
            for r in range(widths[t] // P):
                for c in range(SIDE):
                    rows = slice(c * ROWS, (c + 1) * ROWS)
                    cols = slice(r * P, (r + 1) * P)
                    nc.tensor.matmul_mx(
                        out=sums[t, c][:, r, :],
                        lhsT=codes[t][rows, cols].bitcast(FP8X4),
                        lhsT_scale=scales[t][rows, cols],
                        rhs=s_codes[g][rows, :].bitcast(FP8X4),
                        rhs_scale=s_scales[g][rows, :],
                        start=True,
                        stop=True,
                    )

        def invert(t):
            for c in range(SIDE):
                nc.vector.reciprocal(out=inverse[t, c][:], in_=sums[t, c][:, 0 : widths[t] // P, E - 1])

        def store(t, c):
            g, n0, width = CHUNKS[t]
            rows_out = out[g * SIDE + c, n0 : n0 + width, :].rearrange("(m r) e -> m r e", m=P)
            nc.sync.dma_start(out=rows_out, in_=result[t, c][:])

        def divide_on_scalar(t, c):
            for r in range(widths[t] // P):
                nc.scalar.activation(out=result[t, c][:, r, :], in_=sums[t, c][:, r, :], func=ACT.Copy, scale=inverse[t, c][:, r : r + 1])
            store(t, c)

        def divide_on_vector(t, c):
            deal = widths[t] // P
            nc.vector.tensor_tensor(
                out=result[t, c][:], in0=sums[t, c][:, 0:deal, :], in1=inverse[t, c][:].unsqueeze(2).to_broadcast([P, deal, E]), op=ALU.mult
            )
            store(t, c)

        line_on_scalar(0, 0)
        line_on_vector(0, 1)
        clamp(0, 0)
        line_on_scalar(0, 2)
        clamp(0, 1)
        line_on_vector(0, 3)
        clamp(0, 2)
        clamp(0, 3)
        interleave_state(0)

        for t in (0, 1):
            for j in range(PACK):
                line_on_scalar(t + 1, j)
            interleave(t)
            clamp(t + 1, 0)
            if t == 0:
                quantize_state(0)
            else:
                invert(t - 1)
            quantize(t)
            multiply(t)
            for j in range(1, PACK):
                clamp(t + 1, j)
        interleave_state(1)

        for t in (2, 3):
            divide_on_scalar(0, t - 2)
            line_on_vector(t + 1, 0)
            for j in range(1, PACK):
                line_on_scalar(t + 1, j)
            if t == 2:
                quantize_state(1)
            interleave(t)
            for j in range(PACK):
                clamp(t + 1, j)
            quantize(t)
            multiply(t)
            invert(t - 1)

        for t in (1, 2):
            for c in range(SIDE):
                divide_on_scalar(t, c)
        interleave(4)
        quantize(4)
        multiply(4)
        for t in (3, 4):
            invert(t)
            divide_on_vector(t, 0)
            divide_on_scalar(t, 1)
